import numpy as np
import ml_dtypes


def mxq(x, axis, fmt="e4m3"):
    dtype, down = {"e4m3": (ml_dtypes.float8_e4m3fn, 7), "e5m2": (ml_dtypes.float8_e5m2, 14)}[fmt]
    v = np.moveaxis(np.asarray(x, np.float32).astype(ml_dtypes.bfloat16).astype(np.float64), axis, -1)
    blocks = v.reshape(v.shape[:-1] + (-1, 32))
    amax = np.abs(blocks).max(-1, keepdims=True)
    byte = np.maximum(np.where(amax > 0, np.frexp(amax)[1] - 1 + 127, 0) - down, 1)
    scale = np.exp2(byte - 127.0)
    codes = (blocks / scale).astype(np.float32).astype(dtype).astype(np.float64)
    return np.moveaxis((codes * scale).reshape(v.shape), -1, axis)


WIDE = False


def mx_kscale(k):
    if not WIDE:
        return np.ones(k)
    levels = np.array([10, -10, 5, -5, 0])
    if k % 512:
        return np.exp2(np.random.permutation(np.resize(levels, k // 32))).repeat(32)
    a = np.empty((k // 512, 16))
    for p in range(k // 512):
        a[p, :8] = np.random.permutation(np.resize(levels, 8))
        for g in range(8):
            far = levels[np.abs(levels - a[p, g]) >= 10]
            a[p, g + 8] = far[np.random.randint(len(far))]
    return np.exp2(a.ravel()).repeat(32)


def f64(x):
    return np.asarray(x).astype(np.float64)


def striped(idx):
    return np.tile(idx.reshape(-1, 16).T, (8, 1)).astype(np.uint16)


def unstriped(offs):
    return offs[:16].T.reshape(-1).astype(np.int64)


def pack_weight(w):
    k, n = w.shape
    w = f64(np.asarray(w, np.float32).astype(ml_dtypes.bfloat16)).reshape(k // 32, 32, n)
    amax = np.abs(w).max(1)
    byte = np.clip(np.where(amax > 0, np.frexp(amax)[1] - 1 + 127 - 7, 1), 1, 254)
    scaled = (w * np.exp2(127.0 - byte)[:, None, :]).reshape(k, n).astype(np.float32)
    words = np.ascontiguousarray(scaled.reshape(k // 512, 128, 4, n).transpose(0, 1, 3, 2)).astype(ml_dtypes.float8_e4m3fn).view(np.uint8)
    return words, np.ascontiguousarray(byte.astype(np.uint8).reshape(k // 512, 16, n))


def unpack_weight(words, scales):
    g, p, n, _ = words.shape
    vals = np.ascontiguousarray(words).view(ml_dtypes.float8_e4m3fn).astype(np.float64) * np.repeat(np.exp2(scales.astype(np.float64) - 127.0), 8, axis=1)[..., None]
    return vals.transpose(0, 1, 3, 2).reshape(g * 512, n)


K, T, S, D, N, V = 512, 4096, 1024, 4, 128, 256
P = 2 ** 7


def setup_inputs():
    n = np.random.standard_normal
    s = mx_kscale(K)[:, None]
    packed_xT = pack_weight(n((K, T)) * s)
    return {
        "x_words": packed_xT[0],
        "x_scales": packed_xT[1],
        "w1": (n((K, N)) / np.sqrt(K) / s).astype(np.float32),
        "w2": (n((K, N)) / np.sqrt(K) / s).astype(np.float32),
        "w3": (n((K, N)) / np.sqrt(K) / s).astype(np.float32),
        "core": (np.tile(np.random.uniform(0.3, 1.5, S), (P, 1))).astype(np.float32),
        "bgd": (n((N, V))).astype(np.float32),
        "offs": striped(np.random.permutation(T)[:S]),
    }


def reference(x_words, x_scales, w1, w2, w3, core, bgd, offs):
    xq = unpack_weight(x_words, x_scales)[:, unstriped(offs)]
    cir = mxq(f64(w3), 0, "e4m3").T @ xq
    dx = mxq(f64(w1), 0, "e4m3").T @ xq
    dy = mxq(f64(w2), 0, "e4m3").T @ xq
    rsq = (dx) ** 2 + (dy) ** 2 + 0.05
    kr = (cir * (-1.0 * (np.exp(-1.0 * (rsq * f64(core)[:1]))) + 1.0)) / rsq
    ku = -1.0 * (kr * dy)
    uu = ku.reshape(len(ku), -1, D).sum(axis=2)
    return uu + 0.5 * f64(bgd)

@@ -1,0 +1,199 @@
+from contextlib import ExitStack
+
+import concourse.mybir as mybir
+from concourse.masks import make_identity
+
+K, T, S, D, N, V = 512, 4096, 1024, 4, 128, 256
+FLOPS = 3 * 2 * K * N * S
+
+F32 = mybir.dt.float32
+BF16 = mybir.dt.bfloat16
+I32 = mybir.dt.int32
+U32 = mybir.dt.uint32
+U16 = mybir.dt.uint16
+U8 = mybir.dt.uint8
+FP8X4 = mybir.dt.float8_e4m3fn_x4
+ACT = mybir.ActivationFunctionType
+ALU = mybir.AluOpType
+
+P = 128
+PACK = 4
+HALVES = V // P
+PAIRS = HALVES * D // 2
+
+
+def tile_picked_ybiot_vel_p_kernel(
+    tc, x_words, x_scales, w1, w2, w3, core, bgd, offs, out
+):
+    nc = tc.nc
+    with ExitStack() as ctx:
+        keep = ctx.enter_context(tc.tile_pool(name="keep", bufs=1))
+        psum = ctx.enter_context(tc.psum_pool(name="psum", bufs=1))
+
+        offsets = keep.tile([P, S // 16], U16, name="offsets")
+        nc.sync.dma_start(offsets[:], offs)
+
+        byte_table = keep.tile([P, T], U8, name="byte_table", align_bytes=64)
+        for r in range(2):
+            nc.sync.dma_start(byte_table[r:32:2, :].bitcast(I32), x_scales[0].bitcast(I32))
+        nc.vector.memset(byte_table[64:P, :].bitcast(I32), 0)
+        nc.vector.memset(byte_table[32:64, :].bitcast(I32), 0)
+
+        w_raw = []
+        for i, w in enumerate((w1, w2)):
+            raw = keep.tile([P, PACK, N], F32, name="w_raw%d" % i)
+            nc.sync.dma_start(raw[:], w.rearrange("(p j) n -> p j n", j=PACK))
+            w_raw.append(raw)
+        word_table = keep.tile([P, T], U32, name="word_table", align_bytes=64)
+        nc.sync.dma_start(
+            word_table[:].bitcast(I32),
+            x_words[0].rearrange("p c r -> p (c r)").bitcast(I32),
+        )
+        raw = keep.tile([P, PACK, N], F32, name="w_raw2", tag="late")
+        nc.sync.dma_start(raw[:], w3.rearrange("(p j) n -> p j n", j=PACK))
+        w_raw.append(raw)
+        core_t = keep.tile([P, HALVES, 2 * D], F32, name="core_t")
+        nc.sync.dma_start(
+            core_t[:, :, 0:D], core[0].rearrange("(h p d) -> p h d", h=HALVES, d=D)
+        )
+
+        ident = keep.tile([P, P], F32, name="ident")
+        make_identity(nc, ident[:])
+
+        x_plane = keep.tile([P, S], U8, name="x_plane", align_bytes=64)
+        nc.gpsimd.memset(x_plane[:].bitcast(I32), 0)
+        bytes_picked = keep.tile([P, S], U8, name="bytes_picked", align_bytes=64)
+        nc.vector.tensor_copy(bytes_picked[:], byte_table[:].indirect(offsets[:]))
+        bytes_dealt = keep.tile([P, S], U8, name="bytes_dealt", align_bytes=64)
+        nc.vector.tensor_copy(
+            bytes_dealt[:].rearrange("p (h d v) -> p h d v", h=HALVES, d=D),
+            bytes_picked[:].rearrange("p (h v d) -> p h d v", h=HALVES, d=D),
+        )
+        for q in range(4):
+            nc.scalar.dma_start(
+                x_plane[32 * q : 32 * q + 4, :].bitcast(I32),
+                bytes_dealt[8 * q : 8 * q + 8 : 2, :].bitcast(I32),
+            )
+
+        w_bf = []
+        for i in range(3):
+            if i != 1:
+                grouped = keep.tile(
+                    [P, (2 - i // 2) * N, PACK], BF16, name="w_bf%d" % i, align_bytes=64
+                )
+                w_bf.append(grouped)
+            lo = N * (i % 2)
+            nc.scalar.activation(
+                grouped[:, lo : lo + N, :], w_raw[i][:].rearrange("p j n -> p n j"), ACT.Copy
+            )
+        w_codes, w_plane = [], []
+        for i, width in enumerate((2 * N, N)):
+            codes = keep.tile([P, width], U32, name="w_codes%d" % i, align_bytes=64)
+            plane = keep.tile([P, width], U8, name="w_plane%d" % i, align_bytes=64)
+            nc.vector.quantize_mx(
+                out=codes[:].bitcast(FP8X4),
+                scales=plane[:],
+                in_=w_bf[i][:].rearrange("p n j -> p (n j)"),
+            )
+            w_codes.append(codes)
+            w_plane.append(plane)
+
+        neg_core = keep.tile([P, HALVES, D], F32, name="neg_core")
+        nc.vector.tensor_scalar_mul(neg_core[:], core_t[:, :, 0:D], -1.0)
+        bgd_t = keep.tile([P, V], F32, name="bgd_t", tag="late")
+        nc.sync.dma_start(bgd_t[:], bgd)
+
+        x_codes = []
+        for h in range(HALVES):
+            codes = keep.tile([P, D, P], U32, name="x_codes%d" % h, align_bytes=64)
+            cols = slice(h * (P * D // 16), (h + 1) * (P * D // 16))
+            nc.vector.tensor_copy(
+                codes[:].rearrange("p d v -> p v d"), word_table[:].indirect(offsets[:, cols])
+            )
+            x_codes.append(codes)
+
+        def product(dst, h, d, i):
+            lo = (h * D + d) * P
+            nc.tensor.matmul_mx(
+                out=dst,
+                lhsT=x_codes[h][:, d, :].bitcast(FP8X4),
+                lhsT_scale=x_plane[:, lo : lo + P],
+                rhs=w_codes[i][:].bitcast(FP8X4),
+                rhs_scale=w_plane[i][:],
+                start=True,
+                stop=True,
+            )
+
+        disp, circ = [], []
+        for h in range(HALVES):
+            for r in range(2):
+                bank = psum.tile([P, 2, 2 * N], F32, name="disp%d" % (2 * h + r))
+                for c in range(2):
+                    product(bank[:, c, :], h, 2 * r + c, 0)
+                disp.append(bank)
+        for h in range(HALVES):
+            bank = psum.tile([P, D, N], F32, name="circ%d" % h)
+            for d in range(D):
+                product(bank[:, d, :], h, d, 1)
+            circ.append(bank)
+
+        squares = []
+        for h in range(HALVES):
+            sq = keep.tile([P, D, 2 * N], F32, name="squares%d" % h, tag="sq%d" % h)
+            for r in range(2):
+                nc.scalar.activation(sq[:, 2 * r : 2 * r + 2, :], disp[2 * h + r][:], ACT.Square)
+            squares.append(sq)
+
+        rsq, numer = [], []
+        for q in range(PAIRS):
+            h, r = divmod(q, 2)
+            t = keep.tile([P, 2, N], F32, name="rsq%d" % q)
+            part = squares[h][:, 2 * r : 2 * r + 2, :]
+            nc.vector.scalar_tensor_tensor(
+                t[:], part[:, :, 0:N], 0.05, part[:, :, N : 2 * N], ALU.add, ALU.add
+            )
+            rsq.append(t)
+        for q in range(PAIRS):
+            h, r = divmod(q, 2)
+            decay = keep.tile([P, 2, N], F32, name="decay%d" % q)
+            for c in range(2):
+                d = 2 * r + c
+                nc.scalar.activation(
+                    decay[:, c, :], rsq[q][:, c, :], ACT.Exp, scale=neg_core[:, h, d : d + 1]
+                )
+            by_dy = keep.tile([P, 2, N], F32, name="by_dy%d" % q)
+            nc.vector.scalar_tensor_tensor(
+                by_dy[:], decay[:], -1.0, disp[q][:, :, N : 2 * N], ALU.add, ALU.mult
+            )
+            t = keep.tile([P, 2, N], F32, name="numer%d" % q)
+            nc.vector.tensor_tensor(t[:], by_dy[:], circ[h][:, 2 * r : 2 * r + 2, :], ALU.mult)
+            numer.append(t)
+
+        inv_r = keep.tile([P, PAIRS, 2, N], F32, name="inv_r", tag="sq1")
+        for h in range(HALVES):
+            acc = psum.tile([P, P], F32, name="acc%d" % h)
+            for r in range(2):
+                q = 2 * h + r
+                nc.scalar.activation(inv_r[:, q], rsq[q][:], ACT.Abs_reciprocal_sqrt)
+                ku = keep.tile([P, 2, N], F32, name="ku%d" % q)
+                step = keep.tile([P, 2, N], F32, name="step%d" % q)
+                if h == 0:
+                    nc.vector.tensor_tensor(step[:], numer[q][:], inv_r[:, q], ALU.mult)
+                    nc.vector.tensor_tensor(ku[:], step[:], inv_r[:, q], ALU.mult)
+                else:
+                    nc.scalar.activation(step[:], inv_r[:, q], ACT.Square)
+                    nc.vector.tensor_tensor(ku[:], numer[q][:], step[:], ALU.mult)
+                for c in range(2):
+                    nc.tensor.matmul(
+                        acc[:],
+                        lhsT=ku[:, c, :],
+                        rhs=ident[:],
+                        start=(r == 0 and c == 0),
+                        stop=(r == 1 and c == 1),
+                        is_transpose=True,
+                    )
+            res = keep.tile([P, P], F32, name="res%d" % h)
+            nc.vector.scalar_tensor_tensor(
+                res[:], bgd_t[:, h * P : (h + 1) * P], 0.5, acc[:], ALU.mult, ALU.add
+            )
+            nc.sync.dma_start(out[:, h * P : (h + 1) * P], res[:])

@@ -57,11 +57,16 @@ def tile_picked_ybiot_vel_p_kernel(
             core_t[:, :, 0:D], core[0].rearrange("(h p d) -> p h d", h=HALVES, d=D)
         )
 
+        one = keep.tile([P, 1], F32, name="one")
+        nc.vector.memset(one[:], 1.0)
+        warm = keep.tile([P, 1], F32, name="warm")
+        nc.scalar.activation(warm[:], one[:], ACT.Abs_reciprocal_sqrt)
+
         ident = keep.tile([P, P], F32, name="ident")
         make_identity(nc, ident[:])
 
         x_plane = keep.tile([P, S], U8, name="x_plane", align_bytes=64)
-        nc.gpsimd.memset(x_plane[:].bitcast(I32), 0)
+        nc.vector.memset(x_plane[:].bitcast(I32), 0)
         bytes_picked = keep.tile([P, S], U8, name="bytes_picked", align_bytes=64)
         nc.vector.tensor_copy(bytes_picked[:], byte_table[:].indirect(offsets[:]))
         bytes_dealt = keep.tile([P, S], U8, name="bytes_dealt", align_bytes=64)
@@ -83,9 +88,7 @@ def tile_picked_ybiot_vel_p_kernel(
                 )
                 w_bf.append(grouped)
             lo = N * (i % 2)
-            nc.scalar.activation(
-                grouped[:, lo : lo + N, :], w_raw[i][:].rearrange("p j n -> p n j"), ACT.Copy
-            )
+            nc.scalar.copy(grouped[:, lo : lo + N, :], w_raw[i][:].rearrange("p j n -> p n j"))
         w_codes, w_plane = [], []
         for i, width in enumerate((2 * N, N)):
             codes = keep.tile([P, width], U32, name="w_codes%d" % i, align_bytes=64)
@@ -124,76 +127,124 @@ def tile_picked_ybiot_vel_p_kernel(
                 stop=True,
             )
 
+        groups = [(0, 1), (1, 2), (2, 4), (4, 6), (6, 8)]
         disp, circ = [], []
-        for h in range(HALVES):
-            for r in range(2):
-                bank = psum.tile([P, 2, 2 * N], F32, name="disp%d" % (2 * h + r))
-                for c in range(2):
-                    product(bank[:, c, :], h, 2 * r + c, 0)
-                disp.append(bank)
-        for h in range(HALVES):
+
+        def displacements(g):
+            lo, hi = groups[g]
+            bank = psum.tile([P, hi - lo, 2 * N], F32, name="disp%d" % g, tag="bank%d" % g)
+            for t in range(lo, hi):
+                product(bank[:, t - lo, :], t // D, t % D, 0)
+            disp.append(bank)
+
+        def circulations(h):
             bank = psum.tile([P, D, N], F32, name="circ%d" % h)
             for d in range(D):
                 product(bank[:, d, :], h, d, 1)
             circ.append(bank)
 
-        squares = []
+        for g in range(5):
+            displacements(g)
         for h in range(HALVES):
-            sq = keep.tile([P, D, 2 * N], F32, name="squares%d" % h, tag="sq%d" % h)
-            for r in range(2):
-                nc.scalar.activation(sq[:, 2 * r : 2 * r + 2, :], disp[2 * h + r][:], ACT.Square)
-            squares.append(sq)
+            circulations(h)
 
-        rsq, numer = [], []
-        for q in range(PAIRS):
-            h, r = divmod(q, 2)
-            t = keep.tile([P, 2, N], F32, name="rsq%d" % q)
-            part = squares[h][:, 2 * r : 2 * r + 2, :]
-            nc.vector.scalar_tensor_tensor(
-                t[:], part[:, :, 0:N], 0.05, part[:, :, N : 2 * N], ALU.add, ALU.add
-            )
-            rsq.append(t)
-        for q in range(PAIRS):
-            h, r = divmod(q, 2)
-            decay = keep.tile([P, 2, N], F32, name="decay%d" % q)
-            for c in range(2):
-                d = 2 * r + c
-                nc.scalar.activation(
-                    decay[:, c, :], rsq[q][:, c, :], ACT.Exp, scale=neg_core[:, h, d : d + 1]
-                )
-            by_dy = keep.tile([P, 2, N], F32, name="by_dy%d" % q)
-            nc.vector.scalar_tensor_tensor(
-                by_dy[:], decay[:], -1.0, disp[q][:, :, N : 2 * N], ALU.add, ALU.mult
-            )
-            t = keep.tile([P, 2, N], F32, name="numer%d" % q)
-            nc.vector.tensor_tensor(t[:], by_dy[:], circ[h][:, 2 * r : 2 * r + 2, :], ALU.mult)
-            numer.append(t)
+        TILES = HALVES * D
+        squares = keep.tile([P, TILES, 2 * N], F32, name="squares", tag="squares")
+        rsq = keep.tile([P, TILES, N], F32, name="rsq")
+        root = keep.tile([P, TILES, N], F32, name="root")
+        first = keep.tile([P, TILES, N], F32, name="first")
+        second = keep.tile([P, TILES, N], F32, name="second")
+        swirl = keep.tile([P, TILES, N], F32, name="swirl")
 
-        inv_r = keep.tile([P, PAIRS, 2, N], F32, name="inv_r", tag="sq1")
-        for h in range(HALVES):
-            acc = psum.tile([P, P], F32, name="acc%d" % h)
-            for r in range(2):
-                q = 2 * h + r
-                nc.scalar.activation(inv_r[:, q], rsq[q][:], ACT.Abs_reciprocal_sqrt)
-                ku = keep.tile([P, 2, N], F32, name="ku%d" % q)
-                step = keep.tile([P, 2, N], F32, name="step%d" % q)
-                if h == 0:
-                    nc.vector.tensor_tensor(step[:], numer[q][:], inv_r[:, q], ALU.mult)
-                    nc.vector.tensor_tensor(ku[:], step[:], inv_r[:, q], ALU.mult)
-                else:
-                    nc.scalar.activation(step[:], inv_r[:, q], ACT.Square)
-                    nc.vector.tensor_tensor(ku[:], numer[q][:], step[:], ALU.mult)
-                for c in range(2):
-                    nc.tensor.matmul(
-                        acc[:],
-                        lhsT=ku[:, c, :],
-                        rhs=ident[:],
-                        start=(r == 0 and c == 0),
-                        stop=(r == 1 and c == 1),
-                        is_transpose=True,
-                    )
+        def square(g):
+            lo, hi = groups[g]
+            nc.scalar.activation(squares[:, lo:hi, :], disp[g][:], ACT.Square)
+
+        def radius(lo):
+            part = squares[:, lo : lo + 2, :]
+            nc.vector.scalar_tensor_tensor(
+                rsq[:, lo : lo + 2, :], part[:, :, 0:N], 0.05, part[:, :, N : 2 * N], ALU.add, ALU.add
+            )
+
+        def inverse(lo):
+            nc.scalar.activation(
+                root[:, lo : lo + 2, :], rsq[:, lo : lo + 2, :], ACT.Abs_reciprocal_sqrt
+            )
+
+        def times_dy(g, dst, src):
+            lo, hi = groups[g]
+            nc.vector.tensor_tensor(
+                dst[:, lo:hi, :], src[:, lo:hi, :], disp[g][:, :, N : 2 * N], ALU.mult
+            )
+
+        def times_cir(lo, dst, src):
+            nc.vector.tensor_tensor(
+                dst[:, lo : lo + 2, :],
+                src[:, lo : lo + 2, :],
+                circ[lo // D][:, lo % D : lo % D + 2, :],
+                ALU.mult,
+            )
+
+        def times_root(lo):
+            nc.vector.tensor_tensor(
+                second[:, lo : lo + 2, :], first[:, lo : lo + 2, :], root[:, lo : lo + 2, :], ALU.mult
+            )
+
+        square(0)
+        square(1)
+        radius(0)
+        square(2)
+        radius(2)
+        inverse(0)
+        times_dy(0, first, root)
+        times_dy(1, first, root)
+        square(3)
+        radius(4)
+        times_root(0)
+        square(4)
+        radius(6)
+        inverse(2)
+        inverse(4)
+        nc.scalar.activation(second[:, 4:6, :], root[:, 4:6, :], ACT.Square)
+        inverse(6)
+        times_dy(2, first, root)
+        times_cir(0, swirl, second)
+        times_root(2)
+        times_dy(3, first, second)
+        times_cir(2, swirl, second)
+        times_dy(4, first, root)
+        times_cir(4, swirl, first)
+        times_root(6)
+
+        decay = keep.tile([P, TILES, N], F32, name="decay", tag="squares")
+        ku = keep.tile([P, TILES, N], F32, name="ku")
+        acc = [psum.tile([P, P], F32, name="acc%d" % h, tag="bank%d" % h) for h in range(HALVES)]
+
+        def finish(h):
             res = keep.tile([P, P], F32, name="res%d" % h)
             nc.vector.scalar_tensor_tensor(
-                res[:], bgd_t[:, h * P : (h + 1) * P], 0.5, acc[:], ALU.mult, ALU.add
+                res[:], bgd_t[:, h * P : (h + 1) * P], 0.5, acc[h][:], ALU.mult, ALU.add
             )
             nc.sync.dma_start(out[:, h * P : (h + 1) * P], res[:])
+
+        for lo, hi in [(t, t + 1) for t in range(TILES)]:
+            for t in range(lo, hi):
+                nc.scalar.activation(
+                    decay[:, t, :], rsq[:, t, :], ACT.Exp, scale=neg_core[:, t // D, t % D : t % D + 1]
+                )
+            nc.vector.scalar_tensor_tensor(
+                ku[:, lo:hi, :], decay[:, lo:hi, :], -1.0, swirl[:, lo:hi, :], ALU.add, ALU.mult
+            )
+            if lo == 0:
+                times_cir(6, swirl, second)
+            for t in range(lo, hi):
+                nc.tensor.matmul(
+                    acc[t // D][:],
+                    lhsT=ku[:, t, :],
+                    rhs=ident[:],
+                    start=(t % D == 0),
+                    stop=(t % D == D - 1),
+                    is_transpose=True,
+                )
+        finish(0)
+        finish(1)

from contextlib import ExitStack

import concourse.mybir as mybir
from concourse.masks import make_identity

K, T, S, D, N, V = 512, 4096, 1024, 4, 128, 256
FLOPS = 3 * 2 * K * N * S

F32 = mybir.dt.float32
BF16 = mybir.dt.bfloat16
I32 = mybir.dt.int32
U32 = mybir.dt.uint32
U16 = mybir.dt.uint16
U8 = mybir.dt.uint8
FP8X4 = mybir.dt.float8_e4m3fn_x4
ACT = mybir.ActivationFunctionType
ALU = mybir.AluOpType

P = 128
PACK = 4
HALVES = V // P
PAIRS = HALVES * D // 2


def tile_picked_ybiot_vel_p_kernel(
    tc, x_words, x_scales, w1, w2, w3, core, bgd, offs, out
):
    nc = tc.nc
    with ExitStack() as ctx:
        keep = ctx.enter_context(tc.tile_pool(name="keep", bufs=1))
        psum = ctx.enter_context(tc.psum_pool(name="psum", bufs=1))

        offsets = keep.tile([P, S // 16], U16, name="offsets")
        nc.sync.dma_start(offsets[:], offs)

        byte_table = keep.tile([P, T], U8, name="byte_table", align_bytes=64)
        for r in range(2):
            nc.sync.dma_start(byte_table[r:32:2, :].bitcast(I32), x_scales[0].bitcast(I32))
        nc.vector.memset(byte_table[64:P, :].bitcast(I32), 0)
        nc.vector.memset(byte_table[32:64, :].bitcast(I32), 0)

        w_raw = []
        for i, w in enumerate((w1, w2)):
            raw = keep.tile([P, PACK, N], F32, name="w_raw%d" % i)
            nc.sync.dma_start(raw[:], w.rearrange("(p j) n -> p j n", j=PACK))
            w_raw.append(raw)
        word_table = keep.tile([P, T], U32, name="word_table", align_bytes=64)
        nc.sync.dma_start(
            word_table[:].bitcast(I32),
            x_words[0].rearrange("p c r -> p (c r)").bitcast(I32),
        )
        raw = keep.tile([P, PACK, N], F32, name="w_raw2", tag="late")
        nc.sync.dma_start(raw[:], w3.rearrange("(p j) n -> p j n", j=PACK))
        w_raw.append(raw)
        core_t = keep.tile([P, HALVES, 2 * D], F32, name="core_t")
        nc.sync.dma_start(
            core_t[:, :, 0:D], core[0].rearrange("(h p d) -> p h d", h=HALVES, d=D)
        )

        one = keep.tile([P, 1], F32, name="one")
        nc.vector.memset(one[:], 1.0)
        warm = keep.tile([P, 1], F32, name="warm")
        nc.scalar.activation(warm[:], one[:], ACT.Abs_reciprocal_sqrt)

        ident = keep.tile([P, P], F32, name="ident")
        make_identity(nc, ident[:])

        x_plane = keep.tile([P, S], U8, name="x_plane", align_bytes=64)
        nc.vector.memset(x_plane[:].bitcast(I32), 0)
        bytes_picked = keep.tile([P, S], U8, name="bytes_picked", align_bytes=64)
        nc.vector.tensor_copy(bytes_picked[:], byte_table[:].indirect(offsets[:]))
        bytes_dealt = keep.tile([P, S], U8, name="bytes_dealt", align_bytes=64)
        nc.vector.tensor_copy(
            bytes_dealt[:].rearrange("p (h d v) -> p h d v", h=HALVES, d=D),
            bytes_picked[:].rearrange("p (h v d) -> p h d v", h=HALVES, d=D),
        )
        for q in range(4):
            nc.scalar.dma_start(
                x_plane[32 * q : 32 * q + 4, :].bitcast(I32),
                bytes_dealt[8 * q : 8 * q + 8 : 2, :].bitcast(I32),
            )

        w_bf = []
        for i in range(3):
            if i != 1:
                grouped = keep.tile(
                    [P, (2 - i // 2) * N, PACK], BF16, name="w_bf%d" % i, align_bytes=64
                )
                w_bf.append(grouped)
            lo = N * (i % 2)
            nc.scalar.copy(grouped[:, lo : lo + N, :], w_raw[i][:].rearrange("p j n -> p n j"))
        w_codes, w_plane = [], []
        for i, width in enumerate((2 * N, N)):
            codes = keep.tile([P, width], U32, name="w_codes%d" % i, align_bytes=64)
            plane = keep.tile([P, width], U8, name="w_plane%d" % i, align_bytes=64)
            nc.vector.quantize_mx(
                out=codes[:].bitcast(FP8X4),
                scales=plane[:],
                in_=w_bf[i][:].rearrange("p n j -> p (n j)"),
            )
            w_codes.append(codes)
            w_plane.append(plane)

        neg_core = keep.tile([P, HALVES, D], F32, name="neg_core")
        nc.vector.tensor_scalar_mul(neg_core[:], core_t[:, :, 0:D], -1.0)
        bgd_t = keep.tile([P, V], F32, name="bgd_t", tag="late")
        nc.sync.dma_start(bgd_t[:], bgd)

        x_codes = []
        for h in range(HALVES):
            codes = keep.tile([P, D, P], U32, name="x_codes%d" % h, align_bytes=64)
            cols = slice(h * (P * D // 16), (h + 1) * (P * D // 16))
            nc.vector.tensor_copy(
                codes[:].rearrange("p d v -> p v d"), word_table[:].indirect(offsets[:, cols])
            )
            x_codes.append(codes)

        def product(dst, h, d, i):
            lo = (h * D + d) * P
            nc.tensor.matmul_mx(
                out=dst,
                lhsT=x_codes[h][:, d, :].bitcast(FP8X4),
                lhsT_scale=x_plane[:, lo : lo + P],
                rhs=w_codes[i][:].bitcast(FP8X4),
                rhs_scale=w_plane[i][:],
                start=True,
                stop=True,
            )

        groups = [(0, 1), (1, 2), (2, 4), (4, 6), (6, 8)]
        disp, circ = [], []

        def displacements(g):
            lo, hi = groups[g]
            bank = psum.tile([P, hi - lo, 2 * N], F32, name="disp%d" % g, tag="bank%d" % g)
            for t in range(lo, hi):
                product(bank[:, t - lo, :], t // D, t % D, 0)
            disp.append(bank)

        def circulations(h):
            bank = psum.tile([P, D, N], F32, name="circ%d" % h)
            for d in range(D):
                product(bank[:, d, :], h, d, 1)
            circ.append(bank)

        for g in range(5):
            displacements(g)
        for h in range(HALVES):
            circulations(h)

        TILES = HALVES * D
        squares = keep.tile([P, TILES, 2 * N], F32, name="squares", tag="squares")
        rsq = keep.tile([P, TILES, N], F32, name="rsq")
        root = keep.tile([P, TILES, N], F32, name="root")
        first = keep.tile([P, TILES, N], F32, name="first")
        second = keep.tile([P, TILES, N], F32, name="second")
        swirl = keep.tile([P, TILES, N], F32, name="swirl")

        def square(g):
            lo, hi = groups[g]
            nc.scalar.activation(squares[:, lo:hi, :], disp[g][:], ACT.Square)

        def radius(lo):
            part = squares[:, lo : lo + 2, :]
            nc.vector.scalar_tensor_tensor(
                rsq[:, lo : lo + 2, :], part[:, :, 0:N], 0.05, part[:, :, N : 2 * N], ALU.add, ALU.add
            )

        def inverse(lo):
            nc.scalar.activation(
                root[:, lo : lo + 2, :], rsq[:, lo : lo + 2, :], ACT.Abs_reciprocal_sqrt
            )

        def times_dy(g, dst, src):
            lo, hi = groups[g]
            nc.vector.tensor_tensor(
                dst[:, lo:hi, :], src[:, lo:hi, :], disp[g][:, :, N : 2 * N], ALU.mult
            )

        def times_cir(lo, dst, src):
            nc.vector.tensor_tensor(
                dst[:, lo : lo + 2, :],
                src[:, lo : lo + 2, :],
                circ[lo // D][:, lo % D : lo % D + 2, :],
                ALU.mult,
            )

        def times_root(lo):
            nc.vector.tensor_tensor(
                second[:, lo : lo + 2, :], first[:, lo : lo + 2, :], root[:, lo : lo + 2, :], ALU.mult
            )

        square(0)
        square(1)
        radius(0)
        square(2)
        radius(2)
        inverse(0)
        times_dy(0, first, root)
        times_dy(1, first, root)
        square(3)
        radius(4)
        times_root(0)
        square(4)
        radius(6)
        inverse(2)
        inverse(4)
        nc.scalar.activation(second[:, 4:6, :], root[:, 4:6, :], ACT.Square)
        inverse(6)
        times_dy(2, first, root)
        times_cir(0, swirl, second)
        times_root(2)
        times_dy(3, first, second)
        times_cir(2, swirl, second)
        times_dy(4, first, root)
        times_cir(4, swirl, first)
        times_root(6)

        decay = keep.tile([P, TILES, N], F32, name="decay", tag="squares")
        ku = keep.tile([P, TILES, N], F32, name="ku")
        acc = [psum.tile([P, P], F32, name="acc%d" % h, tag="bank%d" % h) for h in range(HALVES)]

        def finish(h):
            res = keep.tile([P, P], F32, name="res%d" % h)
            nc.vector.scalar_tensor_tensor(
                res[:], bgd_t[:, h * P : (h + 1) * P], 0.5, acc[h][:], ALU.mult, ALU.add
            )
            nc.sync.dma_start(out[:, h * P : (h + 1) * P], res[:])

        for lo, hi in [(t, t + 1) for t in range(TILES)]:
            for t in range(lo, hi):
                nc.scalar.activation(
                    decay[:, t, :], rsq[:, t, :], ACT.Exp, scale=neg_core[:, t // D, t % D : t % D + 1]
                )
            nc.vector.scalar_tensor_tensor(
                ku[:, lo:hi, :], decay[:, lo:hi, :], -1.0, swirl[:, lo:hi, :], ALU.add, ALU.mult
            )
            if lo == 0:
                times_cir(6, swirl, second)
            for t in range(lo, hi):
                nc.tensor.matmul(
                    acc[t // D][:],
                    lhsT=ku[:, t, :],
                    rhs=ident[:],
                    start=(t % D == 0),
                    stop=(t % D == D - 1),
                    is_transpose=True,
                )
        finish(0)
        finish(1)
